import numpy as np
import ml_dtypes


def mxq(x, axis, fmt="e4m3"):
    dtype, down = {"e4m3": (ml_dtypes.float8_e4m3fn, 7), "e5m2": (ml_dtypes.float8_e5m2, 14)}[fmt]
    v = np.moveaxis(np.asarray(x, np.float32).astype(ml_dtypes.bfloat16).astype(np.float64), axis, -1)
    blocks = v.reshape(v.shape[:-1] + (-1, 32))
    amax = np.abs(blocks).max(-1, keepdims=True)
    byte = np.maximum(np.where(amax > 0, np.frexp(amax)[1] - 1 + 127, 0) - down, 1)
    scale = np.exp2(byte - 127.0)
    codes = (blocks / scale).astype(np.float32).astype(dtype).astype(np.float64)
    return np.moveaxis((codes * scale).reshape(v.shape), -1, axis)


WIDE = False


def mx_kscale(k):
    if not WIDE:
        return np.ones(k)
    levels = np.array([10, -10, 5, -5, 0])
    if k % 512:
        return np.exp2(np.random.permutation(np.resize(levels, k // 32))).repeat(32)
    a = np.empty((k // 512, 16))
    for p in range(k // 512):
        a[p, :8] = np.random.permutation(np.resize(levels, 8))
        for g in range(8):
            far = levels[np.abs(levels - a[p, g]) >= 10]
            a[p, g + 8] = far[np.random.randint(len(far))]
    return np.exp2(a.ravel()).repeat(32)


def f64(x):
    return np.asarray(x).astype(np.float64)


def striped(idx):
    return np.tile(idx.reshape(-1, 16).T, (8, 1)).astype(np.uint16)


def unstriped(offs):
    return offs[:16].T.reshape(-1).astype(np.int64)


def pack_weight(w):
    k, n = w.shape
    w = f64(np.asarray(w, np.float32).astype(ml_dtypes.bfloat16)).reshape(k // 32, 32, n)
    amax = np.abs(w).max(1)
    byte = np.clip(np.where(amax > 0, np.frexp(amax)[1] - 1 + 127 - 7, 1), 1, 254)
    scaled = (w * np.exp2(127.0 - byte)[:, None, :]).reshape(k, n).astype(np.float32)
    words = np.ascontiguousarray(scaled.reshape(k // 512, 128, 4, n).transpose(0, 1, 3, 2)).astype(ml_dtypes.float8_e4m3fn).view(np.uint8)
    return words, np.ascontiguousarray(byte.astype(np.uint8).reshape(k // 512, 16, n))


def unpack_weight(words, scales):
    g, p, n, _ = words.shape
    vals = np.ascontiguousarray(words).view(ml_dtypes.float8_e4m3fn).astype(np.float64) * np.repeat(np.exp2(scales.astype(np.float64) - 127.0), 8, axis=1)[..., None]
    return vals.transpose(0, 1, 3, 2).reshape(g * 512, n)


K, T, S, D, N, V = 1024, 2048, 512, 4, 256, 128
P = 2 ** 7


def setup_inputs():
    n = np.random.standard_normal
    s = mx_kscale(K)[:, None]
    packed_xT = pack_weight(n((K, T)) * s)
    return {
        "x_words": packed_xT[0],
        "x_scales": packed_xT[1],
        "w1": (n((K, N)) / np.sqrt(K) / s).astype(np.float32),
        "pred": (0.7 * n((N, V))).astype(np.float32),
        "inns": (np.random.uniform(0.5, 2.0, (N, V))).astype(np.float32),
        "miss": (np.tile(np.random.uniform(0.2, 0.9, V), (P, 1))).astype(np.float32),
        "gain": (np.tile(np.random.uniform(0.2, 0.9, V), (P, 1))).astype(np.float32),
        "offs": striped(np.random.permutation(T)[:S]),
    }


def reference(x_words, x_scales, w1, pred, inns, miss, gain, offs):
    xq = unpack_weight(x_words, x_scales)[:, unstriped(offs)]
    y = mxq(f64(w1), 0, "e4m3").T @ xq
    nu = y - (np.repeat(f64(pred), D, axis=1))
    lik = np.exp(-0.5 * (((nu) ** 2) / (np.repeat(f64(inns), D, axis=1))))
    tot = lik.reshape(len(lik), -1, D).sum(axis=2) + f64(miss)[:1]
    beta = lik / np.repeat(tot, D, axis=1)
    bn = beta * nu
    comb = bn.reshape(len(bn), -1, D).sum(axis=2)
    return f64(pred) + f64(gain)[:1] * comb

@@ -1,0 +1,221 @@
+from contextlib import ExitStack
+
+import concourse.mybir as mybir
+from concourse.masks import make_identity
+
+K, T, S, D, N, V = 1024, 2048, 512, 4, 256, 128
+FLOPS = 2 * K * N * S
+
+F32 = mybir.dt.float32
+BF16 = mybir.dt.bfloat16
+I32 = mybir.dt.int32
+U32 = mybir.dt.uint32
+U16 = mybir.dt.uint16
+U8 = mybir.dt.uint8
+FP8X4 = mybir.dt.float8_e4m3fn_x4
+ACT = mybir.ActivationFunctionType
+ALU = mybir.AluOpType
+
+P = 128
+PACK = 4
+PASSES = K // (P * PACK)
+HALVES = N // P
+PAIR = 2
+
+
+def tile_picked_ypdaf_mean_p_kernel(
+    tc, x_words, x_scales, w1, pred, inns, miss, gain, offs, out
+):
+    nc = tc.nc
+    with ExitStack() as ctx:
+        sb = ctx.enter_context(tc.tile_pool(name="sb", bufs=1))
+        ps = ctx.enter_context(tc.psum_pool(name="ps", bufs=1))
+
+        offsets = sb.tile([P, S // 16], U16, name="offsets")
+        inns_sb = sb.tile([P, HALVES, V], F32, name="inns_sb")
+        pred_sb = sb.tile([P, HALVES, V], F32, name="pred_sb")
+        x_bytes = sb.tile([P, T], U8, name="x_bytes", align_bytes=64)
+        gain_col = sb.tile([P, 1], F32, name="gain_col")
+        miss_col = sb.tile([P, 1], F32, name="miss_col")
+        x_tab = [sb.tile([P, T], U32, name=f"x_tab{o}", align_bytes=64) for o in range(PASSES)]
+        w_raw = {(o, h): sb.tile([P, PACK, P], F32, name=f"w_raw{o}{h}") for h in range(HALVES) for o in range(PASSES)}
+
+        nc.vector.memset(x_bytes[:].bitcast(I32), 0)
+        nc.sync.dma_start(inns_sb[:], inns.rearrange("(h p) v -> p h v", p=P))
+        nc.sync.dma_start(offsets[:], offs)
+        nc.sync.dma_start(x_tab[0][:].bitcast(I32), x_words[0].rearrange("p n t -> p (n t)").bitcast(I32))
+        for q in range(4):
+            nc.sync.dma_start(
+                x_bytes[32 * q : 32 * q + 4 * PASSES, :].bitcast(I32), x_scales[:, 4 * q : 4 * q + 4, :].bitcast(I32)
+            )
+        nc.sync.dma_start(x_tab[1][:].bitcast(I32), x_words[1].rearrange("p n t -> p (n t)").bitcast(I32))
+        nc.sync.dma_start(pred_sb[:], pred.rearrange("(h p) v -> p h v", p=P))
+        nc.sync.dma_start(miss_col[:], miss[0:1, :].rearrange("o v -> v o"))
+        nc.sync.dma_start(gain_col[:], gain[0:1, :].rearrange("o v -> v o"))
+        for h in range(HALVES):
+            for o in range(PASSES):
+                nc.sync.dma_start(
+                    w_raw[o, h][:],
+                    w1[o * P * PACK : (o + 1) * P * PACK, h * P : (h + 1) * P].rearrange("(p j) c -> p j c", j=PACK),
+                )
+
+        ident = sb.tile([P, P], F32, name="ident")
+        make_identity(nc, ident[:])
+
+        inv_inns = sb.tile([P, HALVES, V], F32, name="inv_inns")
+        nc.vector.reciprocal(inv_inns[:], inns_sb[:])
+        turned = {}
+        for name, src, tag in (("prec_t", inv_inns, "y2"), ("pred_t", pred_sb, "y3")):
+            bank = ps.tile([P, HALVES, P], F32, name=name + "_ps", tag=tag)
+            for h in range(HALVES):
+                nc.tensor.transpose(bank[:, h, :], src[:, h, :], ident[:])
+            turned[name] = sb.tile([P, HALVES, P], F32, name=name)
+            nc.scalar.copy(turned[name][:], bank[:])
+        prec_t, pred_t = turned["prec_t"], turned["pred_t"]
+
+        tot = [ps.tile([P, V], F32, name=f"tot{h}") for h in range(HALVES)]
+        comb = [ps.tile([P, V], F32, name=f"comb{h}") for h in range(HALVES)]
+        for h in range(HALVES):
+            nc.tensor.matmul(tot[h][:], miss_col[:].to_broadcast([P, P]), ident[:], start=True, stop=False, is_transpose=True)
+
+        x_code = [sb.tile([P, D, V], U32, name=f"x_code{o}", align_bytes=64) for o in range(PASSES)]
+        nc.vector.tensor_copy(x_code[0][:].rearrange("p d v -> p v d"), x_tab[0][:].indirect(offsets[:]))
+        picked_bytes = sb.tile([P, S], U8, name="picked_bytes", align_bytes=64)
+        nc.vector.tensor_copy(picked_bytes[:], x_bytes[:].indirect(offsets[:]))
+        x_scale = sb.tile([P, D, V], U8, name="x_scale", align_bytes=64)
+        nc.vector.tensor_copy(x_scale[:], picked_bytes[:].rearrange("p (v d) -> p d v", d=D))
+        nc.vector.tensor_copy(x_code[1][:].rearrange("p d v -> p v d"), x_tab[1][:].indirect(offsets[:]))
+
+        w_code, w_scale = {}, {}
+
+        def quantise(o, h, on_vector):
+            grouped = sb.tile([P, P, PACK], BF16, name=f"w_bf{o}{h}", align_bytes=64)
+            dst = grouped[:].rearrange("p (c i) j -> p c j i", i=4)
+            src = w_raw[o, h][:].rearrange("p j (c i) -> p c j i", i=4)
+            if on_vector:
+                nc.vector.tensor_copy(dst, src)
+            else:
+                nc.scalar.copy(dst, src)
+            w_code[o, h] = sb.tile([P, P], U32, name=f"w_code{o}{h}", align_bytes=64)
+            w_scale[o, h] = sb.tile([P, P], U8, name=f"w_scale{o}{h}", align_bytes=64)
+            nc.vector.quantize_mx(
+                out=w_code[o, h][:].bitcast(FP8X4), scales=w_scale[o, h][:], in_=grouped[:].rearrange("p c j -> p (c j)")
+            )
+
+        y, nu, sq, expo, lik, bn = {}, {}, {}, {}, {}, {}
+
+        def mx_pass(h, d, o):
+            nc.tensor.matmul_mx(
+                out=y[h, d],
+                lhsT=x_code[o][:, d, :].bitcast(FP8X4),
+                lhsT_scale=x_scale[4 * o : P, d, :],
+                rhs=w_code[o, h][:].bitcast(FP8X4),
+                rhs_scale=w_scale[o, h][:],
+                start=(o == 0),
+                stop=(o == PASSES - 1),
+            )
+
+        def spread(t, h):
+            return t[:, h, :].unsqueeze(1).to_broadcast([P, PAIR, P])
+
+        def square(h, g):
+            sq[h, g] = sb.tile([P, PAIR, P], F32, name=f"sq{h}{g}")
+            nc.scalar.activation(sq[h, g][:], nu[h, g][:], ACT.Square)
+
+        def likelihood(h, g):
+            expo[h, g] = sb.tile([P, PAIR, P], F32, name=f"expo{h}{g}")
+            nc.vector.tensor_tensor(expo[h, g][:], sq[h, g][:], spread(prec_t, h), ALU.mult)
+            lik[h, g] = sb.tile([P, PAIR, P], F32, name=f"lik{h}{g}")
+            nc.scalar.activation(lik[h, g][:], expo[h, g][:], ACT.Exp, scale=-0.5)
+            for i in range(PAIR):
+                last = PAIR * g + i == D - 1
+                nc.tensor.matmul(tot[h][:], lik[h, g][:, i, :], ident[:], start=False, stop=last, is_transpose=True)
+
+        def add_up(h, g):
+            for i in range(PAIR):
+                d = PAIR * g + i
+                nc.tensor.matmul(comb[h][:], bn[h, g][:, i, :], ident[:], start=(d == 0), stop=(d == D - 1), is_transpose=True)
+
+        def weighted(h, g):
+            bn[h, g] = sb.tile([P, PAIR, P], F32, name=f"bn{h}{g}")
+            nc.vector.scalar_tensor_tensor(bn[h, g][:], lik[h, g][:], gain_col[:], nu[h, g][:], ALU.mult, ALU.mult)
+            add_up(h, g)
+
+        gnu = {}
+
+        def gained(h, g):
+            gnu[h, g] = sb.tile([P, PAIR, P], F32, name=f"gnu{h}{g}")
+            nc.scalar.activation(gnu[h, g][:], nu[h, g][:], ACT.Copy, scale=gain_col[:])
+
+        def weighted_pool(h, g):
+            bn[h, g] = sb.tile([P, PAIR, P], F32, name=f"bn{h}{g}")
+            nc.gpsimd.tensor_tensor(bn[h, g][:], lik[h, g][:], gnu[h, g][:], ALU.mult)
+            add_up(h, g)
+
+        inv_tot = [sb.tile([P, V], F32, name=f"inv_tot{h}") for h in range(HALVES)]
+        step = [sb.tile([P, V], F32, name=f"step{h}") for h in range(HALVES)]
+        res = [sb.tile([P, V], F32, name=f"res{h}") for h in range(HALVES)]
+
+        def invert(h, cols):
+            nc.vector.reciprocal(inv_tot[h][:, cols], tot[h][:, cols])
+
+        def scale(h, cols):
+            nc.vector.tensor_tensor(step[h][:, cols], comb[h][:, cols], inv_tot[h][:, cols], ALU.mult)
+
+        def shift(h, cols, adder):
+            adder.tensor_tensor(res[h][:, cols], step[h][:, cols], pred_sb[:, h, cols], ALU.add)
+
+        def store(h):
+            nc.sync.dma_start(out[h * P : (h + 1) * P, :], res[h][:])
+
+        quantise(0, 0, False)
+        for d in range(D):
+            bank = ps.tile([P, P], F32, name=f"y0{d}", tag=f"y{d}")
+            y[0, d] = bank[:]
+            mx_pass(0, d, 0)
+        quantise(1, 0, True)
+        for d in range(D):
+            mx_pass(0, d, 1)
+        quantise(1, 1, True)
+        quantise(0, 1, False)
+        for g in range(2):
+            nu[0, g] = sb.tile([P, PAIR, P], F32, name=f"nu0{g}")
+        for d in range(D):
+            nc.vector.tensor_tensor(nu[0, d // PAIR][:, d % PAIR, :], y[0, d], pred_t[:, 0, :], ALU.subtract)
+            if d % PAIR:
+                square(0, d // PAIR)
+        banks = []
+        for g in range(2):
+            bank = ps.tile([P, PAIR, P], F32, name=f"y1{g}", tag=f"y{g}")
+            banks.append(bank)
+            for i in range(PAIR):
+                y[1, PAIR * g + i] = bank[:, i, :]
+                for o in range(PASSES):
+                    mx_pass(1, PAIR * g + i, o)
+        for g in range(2):
+            nu[1, g] = sb.tile([P, PAIR, P], F32, name=f"nu1{g}")
+            nc.vector.tensor_tensor(nu[1, g][:], banks[g][:], spread(pred_t, 1), ALU.subtract)
+            square(1, g)
+        likelihood(0, 0)
+        likelihood(0, 1)
+        likelihood(1, 0)
+        likelihood(1, 1)
+        gained(1, 0)
+        gained(1, 1)
+        weighted(0, 0)
+        weighted(0, 1)
+        whole = slice(0, V)
+        invert(0, whole)
+        weighted_pool(1, 0)
+        weighted_pool(1, 1)
+        scale(0, whole)
+        shift(0, whole, nc.gpsimd)
+        store(0)
+        parts = [slice(0, V // 2), slice(V // 2, V)]
+        for cols in parts:
+            invert(1, cols)
+        for cols in parts:
+            scale(1, cols)
+        for cols in parts:
+            shift(1, cols, nc.vector)
+        store(1)

@@ -1,7 +1,6 @@
 from contextlib import ExitStack
 
 import concourse.mybir as mybir
-from concourse.masks import make_identity
 
 K, T, S, D, N, V = 1024, 2048, 512, 4, 256, 128
 FLOPS = 2 * K * N * S
@@ -20,7 +19,11 @@ P = 128
 PACK = 4
 PASSES = K // (P * PACK)
 HALVES = N // P
+QUADRANTS = 4
+SCALE_ROWS = 4
 PAIR = 2
+PAIRS = D // PAIR
+LINE = 4
 
 
 def tile_picked_ypdaf_mean_p_kernel(
@@ -29,193 +32,193 @@ def tile_picked_ypdaf_mean_p_kernel(
     nc = tc.nc
     with ExitStack() as ctx:
         sb = ctx.enter_context(tc.tile_pool(name="sb", bufs=1))
+        staged = ctx.enter_context(tc.tile_pool(name="staged", bufs=1))
         ps = ctx.enter_context(tc.psum_pool(name="ps", bufs=1))
 
         offsets = sb.tile([P, S // 16], U16, name="offsets")
         inns_sb = sb.tile([P, HALVES, V], F32, name="inns_sb")
         pred_sb = sb.tile([P, HALVES, V], F32, name="pred_sb")
         x_bytes = sb.tile([P, T], U8, name="x_bytes", align_bytes=64)
-        gain_col = sb.tile([P, 1], F32, name="gain_col")
-        miss_col = sb.tile([P, 1], F32, name="miss_col")
-        x_tab = [sb.tile([P, T], U32, name=f"x_tab{o}", align_bytes=64) for o in range(PASSES)]
-        w_raw = {(o, h): sb.tile([P, PACK, P], F32, name=f"w_raw{o}{h}") for h in range(HALVES) for o in range(PASSES)}
-
         nc.vector.memset(x_bytes[:].bitcast(I32), 0)
         nc.sync.dma_start(inns_sb[:], inns.rearrange("(h p) v -> p h v", p=P))
         nc.sync.dma_start(offsets[:], offs)
-        nc.sync.dma_start(x_tab[0][:].bitcast(I32), x_words[0].rearrange("p n t -> p (n t)").bitcast(I32))
-        for q in range(4):
-            nc.sync.dma_start(
-                x_bytes[32 * q : 32 * q + 4 * PASSES, :].bitcast(I32), x_scales[:, 4 * q : 4 * q + 4, :].bitcast(I32)
-            )
-        nc.sync.dma_start(x_tab[1][:].bitcast(I32), x_words[1].rearrange("p n t -> p (n t)").bitcast(I32))
         nc.sync.dma_start(pred_sb[:], pred.rearrange("(h p) v -> p h v", p=P))
-        nc.sync.dma_start(miss_col[:], miss[0:1, :].rearrange("o v -> v o"))
-        nc.sync.dma_start(gain_col[:], gain[0:1, :].rearrange("o v -> v o"))
-        for h in range(HALVES):
-            for o in range(PASSES):
-                nc.sync.dma_start(
-                    w_raw[o, h][:],
-                    w1[o * P * PACK : (o + 1) * P * PACK, h * P : (h + 1) * P].rearrange("(p j) c -> p j c", j=PACK),
-                )
+        for q in range(QUADRANTS):
+            nc.sync.dma_start(
+                x_bytes[32 * q : 32 * q + SCALE_ROWS * PASSES, :].bitcast(I32),
+                x_scales[:, SCALE_ROWS * q : SCALE_ROWS * (q + 1), :].bitcast(I32),
+            )
 
+        table_bytes, weight_bytes, row_bytes = 4 * T, 4 * PACK * N, 4 * V
+        weights_at = PASSES * table_bytes
+        rows_at = weights_at + PASSES * weight_bytes
+        zeros = staged.tile([P, (rows_at + row_bytes) // 4], F32, name="zeros", align_bytes=64, offset=0)
         ident = sb.tile([P, P], F32, name="ident")
-        make_identity(nc, ident[:])
+        nc.gpsimd.memset(zeros[:, 0:P], 0.0)
+        nc.gpsimd.affine_select(
+            out=ident[:], in_=zeros[:, 0:P], compare_op=ALU.not_equal, fill=1.0, base=0, pattern=[[-1, P]], channel_multiplier=1
+        )
+
+        x_table = {}
+
+        def load_words(o):
+            x_table[o] = staged.tile([P, T], U32, name=f"x_table{o}", align_bytes=64, offset=o * table_bytes)
+            nc.sync.dma_start(x_table[o][:].bitcast(I32), x_words[o].rearrange("p n t -> p (n t)").bitcast(I32))
+
+        load_words(0)
+        track_rows = staged.tile([P, V], F32, name="track_rows", offset=rows_at)
+        nc.gpsimd.memset(track_rows[:], 0.0)
+        nc.scalar.dma_start(track_rows[0:1, :], miss[0:1, :])
+        nc.scalar.dma_start(track_rows[1:2, :], gain[0:1, :])
+        load_words(1)
+        w_raw = {}
+        for o in range(PASSES):
+            w_raw[o] = staged.tile([P, PACK, N], F32, name=f"w_raw{o}", offset=weights_at + weight_bytes * o)
+            nc.sync.dma_start(w_raw[o][:], w1[o * P * PACK : (o + 1) * P * PACK, :].rearrange("(p j) m -> p j m", j=PACK))
 
         inv_inns = sb.tile([P, HALVES, V], F32, name="inv_inns")
         nc.vector.reciprocal(inv_inns[:], inns_sb[:])
-        turned = {}
-        for name, src, tag in (("prec_t", inv_inns, "y2"), ("pred_t", pred_sb, "y3")):
-            bank = ps.tile([P, HALVES, P], F32, name=name + "_ps", tag=tag)
-            for h in range(HALVES):
-                nc.tensor.transpose(bank[:, h, :], src[:, h, :], ident[:])
-            turned[name] = sb.tile([P, HALVES, P], F32, name=name)
-            nc.scalar.copy(turned[name][:], bank[:])
-        prec_t, pred_t = turned["prec_t"], turned["pred_t"]
-
-        tot = [ps.tile([P, V], F32, name=f"tot{h}") for h in range(HALVES)]
-        comb = [ps.tile([P, V], F32, name=f"comb{h}") for h in range(HALVES)]
+        inv_inns_t = ps.tile([P, HALVES, P], F32, name="inv_inns_t", tag="comb1")
         for h in range(HALVES):
-            nc.tensor.matmul(tot[h][:], miss_col[:].to_broadcast([P, P]), ident[:], start=True, stop=False, is_transpose=True)
+            nc.tensor.transpose(inv_inns_t[:, h, :], inv_inns[:, h, :], ident[:])
 
-        x_code = [sb.tile([P, D, V], U32, name=f"x_code{o}", align_bytes=64) for o in range(PASSES)]
-        nc.vector.tensor_copy(x_code[0][:].rearrange("p d v -> p v d"), x_tab[0][:].indirect(offsets[:]))
+        track_ps = ps.tile([P, P], F32, name="track_ps", tag="y10")
+        nc.tensor.transpose(track_ps[:], track_rows[:], ident[:])
+        track_cols = sb.tile([P, 2], F32, name="track_cols")
+        nc.vector.tensor_copy(track_cols[:], track_ps[:, 0:2])
+        miss_col, gain_col = track_cols[:, 0:1], track_cols[:, 1:2]
+        safe_gain = sb.tile([P, 1], F32, name="safe_gain")
+        nc.vector.scalar_tensor_tensor(safe_gain[:], gain_col, 0.0, gain_col, ALU.is_equal, ALU.add)
+        inv_gain = sb.tile([P, 1], F32, name="inv_gain")
+        nc.vector.reciprocal(inv_gain[:], safe_gain[:])
+
+        pred_ps = ps.tile([P, HALVES, P], F32, name="pred_ps", tag="y11")
+        for h in range(HALVES):
+            nc.tensor.transpose(pred_ps[:, h, :], pred_sb[:, h, :], ident[:])
+        gain_pred_t = sb.tile([P, HALVES, P], F32, name="gain_pred_t")
+        nc.scalar.activation(gain_pred_t[:], pred_ps[:], ACT.Copy, scale=gain_col)
+
+        def turn_and_add(total, part, start, stop):
+            nc.tensor.matmul(total, part, ident[:], start=start, stop=stop, is_transpose=True)
+
+        tot = {}
+        for h in range(HALVES):
+            tot[h] = ps.tile([P, V], F32, name=f"tot{h}", tag=f"tot{h}")
+            turn_and_add(tot[h][:], miss_col.to_broadcast([P, P]), True, False)
+
         picked_bytes = sb.tile([P, S], U8, name="picked_bytes", align_bytes=64)
         nc.vector.tensor_copy(picked_bytes[:], x_bytes[:].indirect(offsets[:]))
         x_scale = sb.tile([P, D, V], U8, name="x_scale", align_bytes=64)
         nc.vector.tensor_copy(x_scale[:], picked_bytes[:].rearrange("p (v d) -> p d v", d=D))
-        nc.vector.tensor_copy(x_code[1][:].rearrange("p d v -> p v d"), x_tab[1][:].indirect(offsets[:]))
+        x_code = {}
+        for o in range(PASSES):
+            x_code[o] = sb.tile([P, D, V], U32, name=f"x_code{o}", align_bytes=64)
+            nc.vector.tensor_copy(x_code[o][:].rearrange("p d v -> p v d"), x_table[o][:].indirect(offsets[:]))
 
-        w_code, w_scale = {}, {}
+        w_bf, w_code, w_scale, y = {}, {}, {}, {}
 
-        def quantise(o, h, on_vector):
-            grouped = sb.tile([P, P, PACK], BF16, name=f"w_bf{o}{h}", align_bytes=64)
-            dst = grouped[:].rearrange("p (c i) j -> p c j i", i=4)
-            src = w_raw[o, h][:].rearrange("p j (c i) -> p c j i", i=4)
-            if on_vector:
-                nc.vector.tensor_copy(dst, src)
-            else:
-                nc.scalar.copy(dst, src)
+        def interleave(o, h, copy):
+            w_bf[o, h] = sb.tile([P, P, PACK], BF16, name=f"w_bf{o}{h}", tag=f"w_bf{o}{h}", align_bytes=64)
+            copy(
+                w_bf[o, h][:].rearrange("p (c i) j -> p c j i", i=LINE),
+                w_raw[o][:, :, h * P : (h + 1) * P].rearrange("p j (c i) -> p c j i", i=LINE),
+            )
+
+        def quantise(o, h):
             w_code[o, h] = sb.tile([P, P], U32, name=f"w_code{o}{h}", align_bytes=64)
             w_scale[o, h] = sb.tile([P, P], U8, name=f"w_scale{o}{h}", align_bytes=64)
             nc.vector.quantize_mx(
-                out=w_code[o, h][:].bitcast(FP8X4), scales=w_scale[o, h][:], in_=grouped[:].rearrange("p c j -> p (c j)")
+                out=w_code[o, h][:].bitcast(FP8X4),
+                scales=w_scale[o, h][:],
+                in_=w_bf[o, h][:].rearrange("p c j -> p (c j)"),
             )
 
-        y, nu, sq, expo, lik, bn = {}, {}, {}, {}, {}, {}
-
-        def mx_pass(h, d, o):
+        def mx_pass(h, g, i, o):
+            d = PAIR * g + i
             nc.tensor.matmul_mx(
-                out=y[h, d],
+                out=y[h, g][:, i, :],
                 lhsT=x_code[o][:, d, :].bitcast(FP8X4),
-                lhsT_scale=x_scale[4 * o : P, d, :],
+                lhsT_scale=x_scale[SCALE_ROWS * o : P, d, :],
                 rhs=w_code[o, h][:].bitcast(FP8X4),
                 rhs_scale=w_scale[o, h][:],
                 start=(o == 0),
                 stop=(o == PASSES - 1),
             )
 
-        def spread(t, h):
+        interleave(0, 0, nc.scalar.copy)
+        interleave(0, 1, nc.vector.tensor_copy)
+        for h in range(HALVES):
+            quantise(0, h)
+            for g in range(PAIRS):
+                y[h, g] = ps.tile([P, PAIR, P], F32, name=f"y{h}{g}", tag=f"y{h}{g}")
+                mx_pass(h, g, 0, 0)
+        interleave(1, 0, nc.vector.tensor_copy)
+        interleave(1, 1, nc.scalar.copy)
+        for h in range(HALVES):
+            quantise(1, h)
+            for g in range(PAIRS):
+                mx_pass(h, g, 0, 1)
+                for o in range(PASSES):
+                    mx_pass(h, g, 1, o)
+
+        gain_nu, square, lik, comb = {}, {}, {}, {}
+
+        def over_pair(t, h):
             return t[:, h, :].unsqueeze(1).to_broadcast([P, PAIR, P])
 
-        def square(h, g):
-            sq[h, g] = sb.tile([P, PAIR, P], F32, name=f"sq{h}{g}")
-            nc.scalar.activation(sq[h, g][:], nu[h, g][:], ACT.Square)
+        def innovation(h, g, tag):
+            gain_nu[h, g] = sb.tile([P, PAIR, P], F32, name=f"gain_nu{h}{g}", tag=tag, align_bytes=64)
+            nc.vector.scalar_tensor_tensor(
+                gain_nu[h, g][:], y[h, g][:], gain_col, over_pair(gain_pred_t, h), ALU.mult, ALU.subtract
+            )
+            square[h, g] = sb.tile([P, PAIR, P], F32, name=f"square{h}{g}")
+            nc.scalar.activation(square[h, g][:], gain_nu[h, g][:], ACT.Square, scale=inv_gain[:])
 
         def likelihood(h, g):
-            expo[h, g] = sb.tile([P, PAIR, P], F32, name=f"expo{h}{g}")
-            nc.vector.tensor_tensor(expo[h, g][:], sq[h, g][:], spread(prec_t, h), ALU.mult)
+            distance = sb.tile([P, PAIR, P], F32, name=f"distance{h}{g}")
+            nc.vector.tensor_tensor(distance[:], square[h, g][:], over_pair(inv_inns_t, h), ALU.mult)
             lik[h, g] = sb.tile([P, PAIR, P], F32, name=f"lik{h}{g}")
-            nc.scalar.activation(lik[h, g][:], expo[h, g][:], ACT.Exp, scale=-0.5)
+            nc.scalar.activation(lik[h, g][:], distance[:], ACT.Exp, scale=-0.5)
             for i in range(PAIR):
-                last = PAIR * g + i == D - 1
-                nc.tensor.matmul(tot[h][:], lik[h, g][:, i, :], ident[:], start=False, stop=last, is_transpose=True)
+                turn_and_add(tot[h][:], lik[h, g][:, i, :], False, PAIR * g + i == D - 1)
 
-        def add_up(h, g):
+        def weighted(h, g, engine, tag):
+            product = sb.tile([P, PAIR, P], F32, name=f"product{h}{g}", tag=tag, align_bytes=64)
+            engine.tensor_tensor(product[:], lik[h, g][:], gain_nu[h, g][:], ALU.mult)
+            if g == 0:
+                comb[h] = ps.tile([P, V], F32, name=f"comb{h}", tag=f"comb{h}")
             for i in range(PAIR):
                 d = PAIR * g + i
-                nc.tensor.matmul(comb[h][:], bn[h, g][:, i, :], ident[:], start=(d == 0), stop=(d == D - 1), is_transpose=True)
+                turn_and_add(comb[h][:], product[:, i, :], d == 0, d == D - 1)
 
-        def weighted(h, g):
-            bn[h, g] = sb.tile([P, PAIR, P], F32, name=f"bn{h}{g}")
-            nc.vector.scalar_tensor_tensor(bn[h, g][:], lik[h, g][:], gain_col[:], nu[h, g][:], ALU.mult, ALU.mult)
-            add_up(h, g)
-
-        gnu = {}
-
-        def gained(h, g):
-            gnu[h, g] = sb.tile([P, PAIR, P], F32, name=f"gnu{h}{g}")
-            nc.scalar.activation(gnu[h, g][:], nu[h, g][:], ACT.Copy, scale=gain_col[:])
-
-        def weighted_pool(h, g):
-            bn[h, g] = sb.tile([P, PAIR, P], F32, name=f"bn{h}{g}")
-            nc.gpsimd.tensor_tensor(bn[h, g][:], lik[h, g][:], gnu[h, g][:], ALU.mult)
-            add_up(h, g)
-
-        inv_tot = [sb.tile([P, V], F32, name=f"inv_tot{h}") for h in range(HALVES)]
-        step = [sb.tile([P, V], F32, name=f"step{h}") for h in range(HALVES)]
-        res = [sb.tile([P, V], F32, name=f"res{h}") for h in range(HALVES)]
-
-        def invert(h, cols):
-            nc.vector.reciprocal(inv_tot[h][:, cols], tot[h][:, cols])
-
-        def scale(h, cols):
-            nc.vector.tensor_tensor(step[h][:, cols], comb[h][:, cols], inv_tot[h][:, cols], ALU.mult)
-
-        def shift(h, cols, adder):
-            adder.tensor_tensor(res[h][:, cols], step[h][:, cols], pred_sb[:, h, cols], ALU.add)
-
-        def store(h):
-            nc.sync.dma_start(out[h * P : (h + 1) * P, :], res[h][:])
-
-        quantise(0, 0, False)
-        for d in range(D):
-            bank = ps.tile([P, P], F32, name=f"y0{d}", tag=f"y{d}")
-            y[0, d] = bank[:]
-            mx_pass(0, d, 0)
-        quantise(1, 0, True)
-        for d in range(D):
-            mx_pass(0, d, 1)
-        quantise(1, 1, True)
-        quantise(0, 1, False)
-        for g in range(2):
-            nu[0, g] = sb.tile([P, PAIR, P], F32, name=f"nu0{g}")
-        for d in range(D):
-            nc.vector.tensor_tensor(nu[0, d // PAIR][:, d % PAIR, :], y[0, d], pred_t[:, 0, :], ALU.subtract)
-            if d % PAIR:
-                square(0, d // PAIR)
-        banks = []
-        for g in range(2):
-            bank = ps.tile([P, PAIR, P], F32, name=f"y1{g}", tag=f"y{g}")
-            banks.append(bank)
-            for i in range(PAIR):
-                y[1, PAIR * g + i] = bank[:, i, :]
-                for o in range(PASSES):
-                    mx_pass(1, PAIR * g + i, o)
-        for g in range(2):
-            nu[1, g] = sb.tile([P, PAIR, P], F32, name=f"nu1{g}")
-            nc.vector.tensor_tensor(nu[1, g][:], banks[g][:], spread(pred_t, 1), ALU.subtract)
-            square(1, g)
+        innovation(0, 0, "w_bf11")
+        innovation(0, 1, "gain_nu01")
+        innovation(1, 0, "gain_nu10")
         likelihood(0, 0)
+        innovation(1, 1, "gain_nu11")
         likelihood(0, 1)
         likelihood(1, 0)
         likelihood(1, 1)
-        gained(1, 0)
-        gained(1, 1)
-        weighted(0, 0)
-        weighted(0, 1)
-        whole = slice(0, V)
-        invert(0, whole)
-        weighted_pool(1, 0)
-        weighted_pool(1, 1)
-        scale(0, whole)
-        shift(0, whole, nc.gpsimd)
-        store(0)
-        parts = [slice(0, V // 2), slice(V // 2, V)]
-        for cols in parts:
-            invert(1, cols)
-        for cols in parts:
-            scale(1, cols)
-        for cols in parts:
-            shift(1, cols, nc.vector)
-        store(1)
+        weighted(0, 0, nc.vector, "product00")
+        weighted(0, 1, nc.vector, "product01")
+        weighted(1, 0, nc.gpsimd, "gain_nu01")
+        weighted(1, 1, nc.gpsimd, "product11")
+
+        inv_tot = [sb.tile([P, V], F32, name=f"inv_tot{h}") for h in range(HALVES)]
+        update = [sb.tile([P, V], F32, name=f"update{h}") for h in range(HALVES)]
+
+        nc.vector.reciprocal(inv_tot[0][:], tot[0][:])
+        nc.vector.tensor_tensor(update[0][:], comb[0][:], inv_tot[0][:], ALU.mult)
+        result0 = sb.tile([P, V], F32, name="result0", tag="gain_nu11", align_bytes=64)
+        nc.gpsimd.tensor_tensor(result0[:], update[0][:], pred_sb[:, 0, :], ALU.add)
+        nc.sync.dma_start(out[0:P, :], result0[:])
+
+        runs = [slice(0, V // 2), slice(V // 2, V)]
+        result1 = sb.tile([P, V], F32, name="result1")
+        for run in runs:
+            nc.vector.reciprocal(inv_tot[1][:, run], tot[1][:, run])
+        for run in runs:
+            nc.vector.tensor_tensor(update[1][:, run], comb[1][:, run], inv_tot[1][:, run], ALU.mult)
+        for run in runs:
+            nc.vector.tensor_tensor(result1[:, run], update[1][:, run], pred_sb[:, 1, run], ALU.add)
+        nc.sync.dma_start(out[P : 2 * P, :], result1[:])

from contextlib import ExitStack

import concourse.mybir as mybir

K, T, S, D, N, V = 1024, 2048, 512, 4, 256, 128
FLOPS = 2 * K * N * S

F32 = mybir.dt.float32
BF16 = mybir.dt.bfloat16
I32 = mybir.dt.int32
U32 = mybir.dt.uint32
U16 = mybir.dt.uint16
U8 = mybir.dt.uint8
FP8X4 = mybir.dt.float8_e4m3fn_x4
ACT = mybir.ActivationFunctionType
ALU = mybir.AluOpType

P = 128
PACK = 4
PASSES = K // (P * PACK)
HALVES = N // P
QUADRANTS = 4
SCALE_ROWS = 4
PAIR = 2
PAIRS = D // PAIR
LINE = 4


def tile_picked_ypdaf_mean_p_kernel(
    tc, x_words, x_scales, w1, pred, inns, miss, gain, offs, out
):
    nc = tc.nc
    with ExitStack() as ctx:
        sb = ctx.enter_context(tc.tile_pool(name="sb", bufs=1))
        staged = ctx.enter_context(tc.tile_pool(name="staged", bufs=1))
        ps = ctx.enter_context(tc.psum_pool(name="ps", bufs=1))

        offsets = sb.tile([P, S // 16], U16, name="offsets")
        inns_sb = sb.tile([P, HALVES, V], F32, name="inns_sb")
        pred_sb = sb.tile([P, HALVES, V], F32, name="pred_sb")
        x_bytes = sb.tile([P, T], U8, name="x_bytes", align_bytes=64)
        nc.vector.memset(x_bytes[:].bitcast(I32), 0)
        nc.sync.dma_start(inns_sb[:], inns.rearrange("(h p) v -> p h v", p=P))
        nc.sync.dma_start(offsets[:], offs)
        nc.sync.dma_start(pred_sb[:], pred.rearrange("(h p) v -> p h v", p=P))
        for q in range(QUADRANTS):
            nc.sync.dma_start(
                x_bytes[32 * q : 32 * q + SCALE_ROWS * PASSES, :].bitcast(I32),
                x_scales[:, SCALE_ROWS * q : SCALE_ROWS * (q + 1), :].bitcast(I32),
            )

        table_bytes, weight_bytes, row_bytes = 4 * T, 4 * PACK * N, 4 * V
        weights_at = PASSES * table_bytes
        rows_at = weights_at + PASSES * weight_bytes
        zeros = staged.tile([P, (rows_at + row_bytes) // 4], F32, name="zeros", align_bytes=64, offset=0)
        ident = sb.tile([P, P], F32, name="ident")
        nc.gpsimd.memset(zeros[:, 0:P], 0.0)
        nc.gpsimd.affine_select(
            out=ident[:], in_=zeros[:, 0:P], compare_op=ALU.not_equal, fill=1.0, base=0, pattern=[[-1, P]], channel_multiplier=1
        )

        x_table = {}

        def load_words(o):
            x_table[o] = staged.tile([P, T], U32, name=f"x_table{o}", align_bytes=64, offset=o * table_bytes)
            nc.sync.dma_start(x_table[o][:].bitcast(I32), x_words[o].rearrange("p n t -> p (n t)").bitcast(I32))

        load_words(0)
        track_rows = staged.tile([P, V], F32, name="track_rows", offset=rows_at)
        nc.gpsimd.memset(track_rows[:], 0.0)
        nc.scalar.dma_start(track_rows[0:1, :], miss[0:1, :])
        nc.scalar.dma_start(track_rows[1:2, :], gain[0:1, :])
        load_words(1)
        w_raw = {}
        for o in range(PASSES):
            w_raw[o] = staged.tile([P, PACK, N], F32, name=f"w_raw{o}", offset=weights_at + weight_bytes * o)
            nc.sync.dma_start(w_raw[o][:], w1[o * P * PACK : (o + 1) * P * PACK, :].rearrange("(p j) m -> p j m", j=PACK))

        inv_inns = sb.tile([P, HALVES, V], F32, name="inv_inns")
        nc.vector.reciprocal(inv_inns[:], inns_sb[:])
        inv_inns_t = ps.tile([P, HALVES, P], F32, name="inv_inns_t", tag="comb1")
        for h in range(HALVES):
            nc.tensor.transpose(inv_inns_t[:, h, :], inv_inns[:, h, :], ident[:])

        track_ps = ps.tile([P, P], F32, name="track_ps", tag="y10")
        nc.tensor.transpose(track_ps[:], track_rows[:], ident[:])
        track_cols = sb.tile([P, 2], F32, name="track_cols")
        nc.vector.tensor_copy(track_cols[:], track_ps[:, 0:2])
        miss_col, gain_col = track_cols[:, 0:1], track_cols[:, 1:2]
        safe_gain = sb.tile([P, 1], F32, name="safe_gain")
        nc.vector.scalar_tensor_tensor(safe_gain[:], gain_col, 0.0, gain_col, ALU.is_equal, ALU.add)
        inv_gain = sb.tile([P, 1], F32, name="inv_gain")
        nc.vector.reciprocal(inv_gain[:], safe_gain[:])

        pred_ps = ps.tile([P, HALVES, P], F32, name="pred_ps", tag="y11")
        for h in range(HALVES):
            nc.tensor.transpose(pred_ps[:, h, :], pred_sb[:, h, :], ident[:])
        gain_pred_t = sb.tile([P, HALVES, P], F32, name="gain_pred_t")
        nc.scalar.activation(gain_pred_t[:], pred_ps[:], ACT.Copy, scale=gain_col)

        def turn_and_add(total, part, start, stop):
            nc.tensor.matmul(total, part, ident[:], start=start, stop=stop, is_transpose=True)

        tot = {}
        for h in range(HALVES):
            tot[h] = ps.tile([P, V], F32, name=f"tot{h}", tag=f"tot{h}")
            turn_and_add(tot[h][:], miss_col.to_broadcast([P, P]), True, False)

        picked_bytes = sb.tile([P, S], U8, name="picked_bytes", align_bytes=64)
        nc.vector.tensor_copy(picked_bytes[:], x_bytes[:].indirect(offsets[:]))
        x_scale = sb.tile([P, D, V], U8, name="x_scale", align_bytes=64)
        nc.vector.tensor_copy(x_scale[:], picked_bytes[:].rearrange("p (v d) -> p d v", d=D))
        x_code = {}
        for o in range(PASSES):
            x_code[o] = sb.tile([P, D, V], U32, name=f"x_code{o}", align_bytes=64)
            nc.vector.tensor_copy(x_code[o][:].rearrange("p d v -> p v d"), x_table[o][:].indirect(offsets[:]))

        w_bf, w_code, w_scale, y = {}, {}, {}, {}

        def interleave(o, h, copy):
            w_bf[o, h] = sb.tile([P, P, PACK], BF16, name=f"w_bf{o}{h}", tag=f"w_bf{o}{h}", align_bytes=64)
            copy(
                w_bf[o, h][:].rearrange("p (c i) j -> p c j i", i=LINE),
                w_raw[o][:, :, h * P : (h + 1) * P].rearrange("p j (c i) -> p c j i", i=LINE),
            )

        def quantise(o, h):
            w_code[o, h] = sb.tile([P, P], U32, name=f"w_code{o}{h}", align_bytes=64)
            w_scale[o, h] = sb.tile([P, P], U8, name=f"w_scale{o}{h}", align_bytes=64)
            nc.vector.quantize_mx(
                out=w_code[o, h][:].bitcast(FP8X4),
                scales=w_scale[o, h][:],
                in_=w_bf[o, h][:].rearrange("p c j -> p (c j)"),
            )

        def mx_pass(h, g, i, o):
            d = PAIR * g + i
            nc.tensor.matmul_mx(
                out=y[h, g][:, i, :],
                lhsT=x_code[o][:, d, :].bitcast(FP8X4),
                lhsT_scale=x_scale[SCALE_ROWS * o : P, d, :],
                rhs=w_code[o, h][:].bitcast(FP8X4),
                rhs_scale=w_scale[o, h][:],
                start=(o == 0),
                stop=(o == PASSES - 1),
            )

        interleave(0, 0, nc.scalar.copy)
        interleave(0, 1, nc.vector.tensor_copy)
        for h in range(HALVES):
            quantise(0, h)
            for g in range(PAIRS):
                y[h, g] = ps.tile([P, PAIR, P], F32, name=f"y{h}{g}", tag=f"y{h}{g}")
                mx_pass(h, g, 0, 0)
        interleave(1, 0, nc.vector.tensor_copy)
        interleave(1, 1, nc.scalar.copy)
        for h in range(HALVES):
            quantise(1, h)
            for g in range(PAIRS):
                mx_pass(h, g, 0, 1)
                for o in range(PASSES):
                    mx_pass(h, g, 1, o)

        gain_nu, square, lik, comb = {}, {}, {}, {}

        def over_pair(t, h):
            return t[:, h, :].unsqueeze(1).to_broadcast([P, PAIR, P])

        def innovation(h, g, tag):
            gain_nu[h, g] = sb.tile([P, PAIR, P], F32, name=f"gain_nu{h}{g}", tag=tag, align_bytes=64)
            nc.vector.scalar_tensor_tensor(
                gain_nu[h, g][:], y[h, g][:], gain_col, over_pair(gain_pred_t, h), ALU.mult, ALU.subtract
            )
            square[h, g] = sb.tile([P, PAIR, P], F32, name=f"square{h}{g}")
            nc.scalar.activation(square[h, g][:], gain_nu[h, g][:], ACT.Square, scale=inv_gain[:])

        def likelihood(h, g):
            distance = sb.tile([P, PAIR, P], F32, name=f"distance{h}{g}")
            nc.vector.tensor_tensor(distance[:], square[h, g][:], over_pair(inv_inns_t, h), ALU.mult)
            lik[h, g] = sb.tile([P, PAIR, P], F32, name=f"lik{h}{g}")
            nc.scalar.activation(lik[h, g][:], distance[:], ACT.Exp, scale=-0.5)
            for i in range(PAIR):
                turn_and_add(tot[h][:], lik[h, g][:, i, :], False, PAIR * g + i == D - 1)

        def weighted(h, g, engine, tag):
            product = sb.tile([P, PAIR, P], F32, name=f"product{h}{g}", tag=tag, align_bytes=64)
            engine.tensor_tensor(product[:], lik[h, g][:], gain_nu[h, g][:], ALU.mult)
            if g == 0:
                comb[h] = ps.tile([P, V], F32, name=f"comb{h}", tag=f"comb{h}")
            for i in range(PAIR):
                d = PAIR * g + i
                turn_and_add(comb[h][:], product[:, i, :], d == 0, d == D - 1)

        innovation(0, 0, "w_bf11")
        innovation(0, 1, "gain_nu01")
        innovation(1, 0, "gain_nu10")
        likelihood(0, 0)
        innovation(1, 1, "gain_nu11")
        likelihood(0, 1)
        likelihood(1, 0)
        likelihood(1, 1)
        weighted(0, 0, nc.vector, "product00")
        weighted(0, 1, nc.vector, "product01")
        weighted(1, 0, nc.gpsimd, "gain_nu01")
        weighted(1, 1, nc.gpsimd, "product11")

        inv_tot = [sb.tile([P, V], F32, name=f"inv_tot{h}") for h in range(HALVES)]
        update = [sb.tile([P, V], F32, name=f"update{h}") for h in range(HALVES)]

        nc.vector.reciprocal(inv_tot[0][:], tot[0][:])
        nc.vector.tensor_tensor(update[0][:], comb[0][:], inv_tot[0][:], ALU.mult)
        result0 = sb.tile([P, V], F32, name="result0", tag="gain_nu11", align_bytes=64)
        nc.gpsimd.tensor_tensor(result0[:], update[0][:], pred_sb[:, 0, :], ALU.add)
        nc.sync.dma_start(out[0:P, :], result0[:])

        runs = [slice(0, V // 2), slice(V // 2, V)]
        result1 = sb.tile([P, V], F32, name="result1")
        for run in runs:
            nc.vector.reciprocal(inv_tot[1][:, run], tot[1][:, run])
        for run in runs:
            nc.vector.tensor_tensor(update[1][:, run], comb[1][:, run], inv_tot[1][:, run], ALU.mult)
        for run in runs:
            nc.vector.tensor_tensor(result1[:, run], update[1][:, run], pred_sb[:, 1, run], ALU.add)
        nc.sync.dma_start(out[P : 2 * P, :], result1[:])
